import numpy as np
import ml_dtypes


def mxq(x, axis, fmt="e4m3"):
    dtype, down = {"e4m3": (ml_dtypes.float8_e4m3fn, 7), "e5m2": (ml_dtypes.float8_e5m2, 14)}[fmt]
    v = np.moveaxis(np.asarray(x, np.float32).astype(ml_dtypes.bfloat16).astype(np.float64), axis, -1)
    blocks = v.reshape(v.shape[:-1] + (-1, 32))
    amax = np.abs(blocks).max(-1, keepdims=True)
    byte = np.maximum(np.where(amax > 0, np.frexp(amax)[1] - 1 + 127, 0) - down, 1)
    scale = np.exp2(byte - 127.0)
    codes = (blocks / scale).astype(np.float32).astype(dtype).astype(np.float64)
    return np.moveaxis((codes * scale).reshape(v.shape), -1, axis)


WIDE = False


def mx_kscale(k):
    if not WIDE:
        return np.ones(k)
    levels = np.array([10, -10, 5, -5, 0])
    if k % 512:
        return np.exp2(np.random.permutation(np.resize(levels, k // 32))).repeat(32)
    a = np.empty((k // 512, 16))
    for p in range(k // 512):
        a[p, :8] = np.random.permutation(np.resize(levels, 8))
        for g in range(8):
            far = levels[np.abs(levels - a[p, g]) >= 10]
            a[p, g + 8] = far[np.random.randint(len(far))]
    return np.exp2(a.ravel()).repeat(32)


def f64(x):
    return np.asarray(x).astype(np.float64)


def striped(idx):
    return np.tile(idx.reshape(-1, 16).T, (8, 1)).astype(np.uint16)


def unstriped(offs):
    return offs[:16].T.reshape(-1).astype(np.int64)


E2M1 = np.array([0.0, 0.5, 1.0, 1.5, 2.0, 3.0, 4.0, 6.0, -0.0, -0.5, -1.0, -1.5, -2.0, -3.0, -4.0, -6.0])


def pack_weight(w, fmt):
    k, n = w.shape
    w = f64(np.asarray(w, np.float32).astype(ml_dtypes.bfloat16)).reshape(k // 32, 32, n)
    amax = np.abs(w).max(1)
    if fmt == "e4m3":
        byte = np.frexp(amax)[1] - 1 + 127 - 7
    else:
        mant, ex = np.frexp(amax / 6.0)
        byte = np.where(mant > 0.5, ex, ex - 1) + 127
    byte = np.clip(np.where(amax > 0, byte, 1), 1, 254)
    scaled = (w * np.exp2(127.0 - byte)[:, None, :]).reshape(k, n).astype(np.float32)
    by_word = np.ascontiguousarray(scaled.reshape(k // 512, 128, 4, n).transpose(0, 1, 3, 2))
    if fmt == "e4m3":
        words = by_word.astype(ml_dtypes.float8_e4m3fn).view(np.uint8)
    else:
        c = by_word.astype(ml_dtypes.float4_e2m1fn).view(np.uint8) & 0xF
        words = (c[..., 0::2] | (c[..., 1::2] << 4)).reshape(k // 512, 128, 2 * n)
    return np.ascontiguousarray(words), np.ascontiguousarray(byte.astype(np.uint8).reshape(k // 512, 16, n))


def unpack_weight(words, scales, fmt):
    g, _, n = scales.shape
    words = np.ascontiguousarray(words).reshape(g, 128, n, -1)
    if fmt == "e4m3":
        vals = words.view(ml_dtypes.float8_e4m3fn).astype(np.float64)
    else:
        nib = np.empty((g, 128, n, 4), np.uint8)
        nib[..., 0::2] = words & 0xF
        nib[..., 1::2] = words >> 4
        vals = E2M1[nib]
    vals = vals * np.repeat(np.exp2(scales.astype(np.float64) - 127.0), 8, axis=1)[..., None]
    return vals.transpose(0, 1, 3, 2).reshape(g * 512, n)


def gelu(v):
    return 0.5 * v * (1.0 + np.tanh(np.sqrt(2.0 / np.pi) * (v + 0.044715 * v**3)))


K, T, S, H, T3, S2, P = 1024, 4096, 1024, 1024, 2048, 512, 512

def setup_inputs():
    n = np.random.standard_normal
    s = mx_kscale(K)[:, None]
    u = mx_kscale(H)[:, None]
    tab_words, tab_scales = pack_weight(n((K, T)) * s, "e4m3")
    tab2_words, tab2_scales = pack_weight(n((H, T3)) / np.sqrt(H) / u, "e4m3")
    w1 = 0.85 * n((K, H)) / np.sqrt(K) / s * u.T
    w4_words, w4_scales = pack_weight(0.85 * n((K, H)) / np.sqrt(K) / s * u.T, "e2m1")
    return {
        "tab_words": tab_words, "tab_scales": tab_scales,
        "offs": striped(np.random.permutation(T)[:S]),
        "tab2_words": tab2_words, "tab2_scales": tab2_scales,
        "offs2": striped(np.random.permutation(T3)[:S2]),
        "pos1": striped(np.random.permutation(S)[:P]),
        "pos2": striped(np.random.permutation(S)[:P]),
        "w1": w1.astype(np.float32),
        "w4_words": w4_words, "w4_scales": w4_scales,
        "temp": np.random.uniform(0.4, 1.6, S2).astype(np.float32),
        "gain": np.random.uniform(2.0, 8.0, S2).astype(np.float32),
        "lim": (0.6 + n((S2, P))).astype(np.float32),
    }

def reference(tab_words, tab_scales, offs, tab2_words, tab2_scales, offs2, pos1, pos2,
              w1, w4_words, w4_scales, temp, gain, lim):
    v = unpack_weight(tab_words, tab_scales, "e4m3")[:, unstriped(offs)]
    v2 = unpack_weight(tab2_words, tab2_scales, "e4m3")[:, unstriped(offs2)]
    w4 = unpack_weight(w4_words, w4_scales, "e2m1")
    f = mxq(f64(w1), 0, "e4m3").T @ v
    res = w4.T @ v
    h = mxq(np.maximum(f, res), 0, "e4m3")
    e = v2.T @ h
    top = e.max(axis=1)
    a = np.exp(f64(temp)[:, None] * (e[:, unstriped(pos1)] - top[:, None]))
    capped = np.minimum(f64(gain)[:, None] * a, f64(lim))
    c = e[:, unstriped(pos2)]
    return capped * c

@@ -1,0 +1,275 @@
+from contextlib import ExitStack
+
+import concourse.mybir as mybir
+
+K, T, S, H, T3, S2, PICK = 1024, 4096, 1024, 1024, 2048, 512, 512
+FLOPS = 2 * 2 * K * H * S + 2 * H * S2 * S
+
+F32 = mybir.dt.float32
+BF16 = mybir.dt.bfloat16
+I32 = mybir.dt.int32
+U32 = mybir.dt.uint32
+U16 = mybir.dt.uint16
+U8 = mybir.dt.uint8
+FP8X4 = mybir.dt.float8_e4m3fn_x4
+FP4X4 = mybir.dt.float4_e2m1fn_x4
+ALU = mybir.AluOpType
+ACT = mybir.ActivationFunctionType
+
+P = 128
+PACK = 4
+PASS = P * PACK
+BANK = 512
+QUADS = 4
+
+
+def tile_list_clause_draft_scores_kernel(
+    tc, tab_words, tab_scales, offs, tab2_words, tab2_scales, offs2, pos1, pos2,
+    w1, w4_words, w4_scales, temp, gain, lim, out,
+):
+    nc = tc.nc
+    with ExitStack() as ctx:
+        keep = ctx.enter_context(tc.tile_pool(name="keep", bufs=1))
+        shared = ctx.enter_context(tc.tile_pool(name="shared", bufs=1))
+        psum = ctx.enter_context(tc.psum_pool(name="psum", bufs=1))
+
+        def held(shape, dtype, name):
+            return keep.tile(shape, dtype, name=name, align_bytes=64)
+
+        def ring(shape, dtype, name, bufs):
+            return keep.tile(shape, dtype, name=name, tag=name, bufs=bufs, align_bytes=64)
+
+        def placed(shape, dtype, name, kib):
+            return shared.tile(shape, dtype, name=name, align_bytes=64, offset=kib * 1024)
+
+        w4_raw = placed([P, 2 * 2 * H], U8, "w4_raw", 16)
+        nc.sync.dma_start(
+            w4_raw[:].bitcast(I32).rearrange("p (a c) -> p a c", a=2),
+            w4_words.bitcast(I32).rearrange("a p c -> p a c"),
+        )
+        idx = keep.tile([P, S // 16], U16, name="idx")
+        nc.sync.dma_start(idx[:], offs)
+        idx2 = keep.tile([P, S2 // 16], U16, name="idx2")
+        nc.sync.dma_start(idx2[:], offs2)
+        p1 = keep.tile([P, PICK // 16], U16, name="p1")
+        nc.sync.dma_start(p1[:], pos1)
+        p2 = keep.tile([P, PICK // 16], U16, name="p2")
+        nc.sync.dma_start(p2[:], pos2)
+
+        temp_sb = held([P, 4], F32, "temp_sb")
+        gain_sb = held([P, 4], F32, "gain_sb")
+        with nc.allow_non_contiguous_dma(reason="one value a row"):
+            nc.sync.dma_start(temp_sb[:], temp.rearrange("(g p) -> p g", p=P))
+            nc.sync.dma_start(gain_sb[:], gain.rearrange("(g p) -> p g", p=P))
+
+        def load_words(words, a, tile):
+            nc.sync.dma_start(tile[:].bitcast(I32), words[a].rearrange("p t i -> p (t i)").bitcast(I32))
+
+        def load_w1(a, b, kib):
+            raw = placed([P, PACK, PASS], F32, "w1_raw%d%d" % (a, b), kib)
+            rows = w1[a * PASS:(a + 1) * PASS, b * PASS:(b + 1) * PASS]
+            nc.sync.dma_start(raw[:], rows.rearrange("(p j) c -> p j c", j=PACK))
+            return raw
+
+        tab = {0: placed([P, T], U32, "tab0", 0)}
+        load_words(tab_words, 0, tab[0])
+
+        tab_sc = placed([P, T], U8, "tab_sc", 40)
+        w4_sc_raw = held([P, 2 * H], U8, "w4_sc_raw")
+        v_sc1 = held([P, S], U8, "v_sc1")
+        nc.gpsimd.memset(w4_sc_raw[64:, :].bitcast(I32), 0)
+        nc.vector.memset(tab_sc[:].bitcast(I32), 0)
+        nc.vector.memset(w4_sc_raw[:64, :].bitcast(I32), 0)
+        nc.vector.memset(v_sc1[:].bitcast(I32), 0)
+        for q in range(QUADS):
+            nc.scalar.dma_start(
+                tab_sc[32 * q:32 * q + 8, :].bitcast(I32), tab_scales[:, 4 * q:4 * q + 4, :].bitcast(I32))
+        for q in range(QUADS):
+            (nc.scalar if q < 2 else nc.gpsimd).dma_start(
+                w4_sc_raw[32 * q:32 * q + 4, :].bitcast(I32).rearrange("p (a c) -> p a c", a=2),
+                w4_scales[:, 4 * q:4 * q + 4, :].bitcast(I32).rearrange("a q c -> q a c"))
+
+        w4 = held([P, 2 * 2 * H], U8, "w4")
+        nc.vector.tensor_copy(
+            w4[:].bitcast(U16).rearrange("p (g t m) -> p g t m", t=PACK, m=P),
+            w4_raw[:].bitcast(U16).rearrange("p (g m t) -> p g t m", t=PACK, m=P))
+        tab[1] = placed([P, T], U32, "tab1", 16)
+        load_words(tab_words, 1, tab[1])
+        v_sc = held([P, S], U8, "v_sc")
+        nc.vector.tensor_copy(v_sc[:], tab_sc[:].indirect(idx[:]))
+        nc.scalar.dma_start(v_sc1[0:100, :].bitcast(I32), v_sc[4:104, :].bitcast(I32))
+        w4_sc = held([P, 2 * H], U8, "w4_sc")
+        nc.vector.tensor_copy(
+            w4_sc[:].rearrange("p (g t m) -> p g t m", t=PACK, m=P),
+            w4_sc_raw[:].rearrange("p (g m t) -> p g t m", t=PACK, m=P))
+
+        v0 = placed([P, S], U32, "v0", 42)
+        nc.vector.tensor_copy(v0[:], tab[0][:].indirect(idx[:]))
+        v = {(0, u): v0[:, u * BANK:(u + 1) * BANK] for u in range(2)}
+        w1_raw = {(0, 0): load_w1(0, 0, 34), (1, 0): load_w1(1, 0, 0), (0, 1): load_w1(0, 1, 8)}
+        for u in range(2):
+            v1 = held([P, BANK], U32, "v1_%d" % u)
+            nc.vector.tensor_copy(v1[:], tab[1][:].indirect(idx[:, 32 * u:32 * (u + 1)]))
+            v[1, u] = v1[:]
+        w1_raw[1, 1] = load_w1(1, 1, 16)
+        tab2_sc = placed([P, T3], U8, "tab2_sc", 24)
+        nc.gpsimd.memset(tab2_sc[:].bitcast(I32), 0)
+        for q in range(QUADS):
+            nc.sync.dma_start(
+                tab2_sc[32 * q:32 * q + 8, :].bitcast(I32), tab2_scales[:, 4 * q:4 * q + 4, :].bitcast(I32))
+
+        w1_q, w1_sc = {}, {}
+
+        def round_w1(a, b, engine_copy, pieces):
+            wb = ring([P, PACK * PASS], BF16, "w1_bf", 4)
+            dst = wb[:].rearrange("p (t m j) -> p m j t", t=PACK, j=PACK)
+            src = w1_raw[a, b][:].rearrange("p j (m t) -> p m j t", t=PACK)
+            step = P // pieces
+            for s in range(pieces):
+                engine_copy(dst[:, s * step:(s + 1) * step], src[:, s * step:(s + 1) * step])
+            return wb
+
+        def quantise_w1(a, b, wb):
+            w1_q[a, b] = held([P, PASS], U32, "w1_q%d%d" % (a, b))
+            w1_sc[a, b] = held([P, PASS], U8, "w1_sc%d%d" % (a, b))
+            nc.vector.quantize_mx(w1_q[a, b][:].bitcast(FP8X4), w1_sc[a, b][:], wb[:])
+
+        res = {}
+        ROUNDED = ((0, 1), (1, 0), (1, 1))
+
+        def packed_bank(b, u, s, weight):
+            bank = psum.tile([P, PACK, P], F32, name="packed_bank", tag="bank", bufs=8)
+            j0 = u * BANK + s * P
+            for a in range(2):
+                for t in range(PACK):
+                    lhsT, lhsT_scale, rhs_scale = weight(a, b, t, j0)
+                    nc.tensor.matmul_mx(
+                        bank[:, t, :], lhsT=lhsT, lhsT_scale=lhsT_scale,
+                        rhs=v[a, u][:, s * P:(s + 1) * P].bitcast(FP8X4), rhs_scale=rhs_scale,
+                        start=(a == 0 and t == 0), stop=(a == 1 and t == PACK - 1))
+            return bank
+
+        def w1_operands(a, b, t, j0):
+            return (w1_q[a, b][:, t * P:(t + 1) * P].bitcast(FP8X4), w1_sc[a, b][:, t * P:(t + 1) * P],
+                    v_sc[4 * a:, j0:j0 + P])
+
+        def w4_operands(a, b, t, j0, width=P):
+            c0 = ((2 * a + b) * PACK + t) * P
+            plane = v_sc if a == 0 else v_sc1
+            return w4[:, 2 * c0:2 * (c0 + P)].bitcast(FP4X4), w4_sc[:, c0:c0 + P], plane[:, j0:j0 + width]
+
+        def rounded(b, u, weight, name):
+            tile = ring([P, PACK * BANK], BF16, name, 3)
+            for s in range(BANK // P):
+                bank = packed_bank(b, u, s, weight)
+                nc.scalar.copy(
+                    tile[:, s * BANK:(s + 1) * BANK].rearrange("p (j t) -> p j t", t=PACK),
+                    bank[:].rearrange("p t j -> p j t"))
+            return tile
+
+        def residual(b, u):
+            if (b, u) in ROUNDED:
+                res[b, u] = rounded(b, u, w4_operands, "res_bf")
+                return
+            res[b, u] = held([P, PACK, BANK], F32, "res%d%d" % (b, u))
+            for t in range(PACK):
+                bank = psum.tile([P, BANK], F32, name="res_bank", tag="bank", bufs=8)
+                for a in range(2):
+                    lhsT, lhsT_scale, rhs_scale = w4_operands(a, b, t, u * BANK, BANK)
+                    nc.tensor.matmul_mx(
+                        bank[:], lhsT=lhsT, lhsT_scale=lhsT_scale,
+                        rhs=v[a, u].bitcast(FP8X4), rhs_scale=rhs_scale, start=(a == 0), stop=(a == 1))
+                nc.scalar.copy(res[b, u][:, t, :], bank[:])
+
+        h_q, h_sc = {}, {}
+
+        def features(b, u):
+            hb = ring([P, PACK * BANK], BF16, "h_bf", 3)
+            if (b, u) in ROUNDED:
+                f = rounded(b, u, w1_operands, "f_bf")
+                for s in range(2):
+                    cols = slice(s * 2 * BANK, (s + 1) * 2 * BANK)
+                    nc.vector.tensor_tensor(hb[:, cols], f[:, cols], res[b, u][:, cols], ALU.max)
+            else:
+                for s in range(BANK // P):
+                    bank = packed_bank(b, u, s, w1_operands)
+                    nc.vector.tensor_tensor(
+                        hb[:, s * BANK:(s + 1) * BANK].rearrange("p (c i t) -> p c t i", i=4, t=PACK),
+                        bank[:].rearrange("p t (c i) -> p c t i", i=4),
+                        res[b, u][:, :, s * P:(s + 1) * P].rearrange("p t (c i) -> p c t i", i=4),
+                        ALU.max)
+            h_q[b, u] = held([P, BANK], U32, "h_q%d%d" % (b, u))
+            h_sc[b, u] = held([P, BANK], U8, "h_sc%d%d" % (b, u))
+            nc.vector.quantize_mx(h_q[b, u][:].bitcast(FP8X4), h_sc[b, u][:], hb[:])
+
+        v2 = {}
+
+        def gather_drafts(b):
+            v2[b] = held([P, S2], U32, "v2_%d" % b)
+            nc.vector.tensor_copy(v2[b][:], tab2[b][:].indirect(idx2[:]))
+
+        e = [held([P, S], F32, "e%d" % g) for g in range(4)]
+        top = [held([P, 4], F32, "top%d" % u) for u in range(2)]
+        bias = held([P, 4], F32, "bias")
+
+        def scores(g, u):
+            bank = psum.tile([P, BANK], F32, name="e_bank", tag="bank", bufs=8)
+            for b in range(2):
+                nc.tensor.matmul_mx(
+                    bank[:], lhsT=v2[b][:, g * P:(g + 1) * P].bitcast(FP8X4),
+                    lhsT_scale=v2_sc[4 * b:, g * P:(g + 1) * P],
+                    rhs=h_q[b, u][:].bitcast(FP8X4), rhs_scale=h_sc[b, u][:],
+                    start=(b == 0), stop=(b == 1))
+            nc.vector.tensor_scalar(
+                e[g][:, u * BANK:(u + 1) * BANK], bank[:], 1.0, top[0][:, g:g + 1] if u == 1 else None,
+                ALU.mult, ALU.max, accum_out=top[u][:, g:g + 1])
+
+        def finish(g):
+            nc.vector.tensor_scalar(
+                bias[:, g:g + 1], top[1][:, g:g + 1], temp_sb[:, g:g + 1], -1.0, ALU.mult, ALU.mult)
+            look = held([P, PICK], F32, "look%d" % g)
+            nc.scalar.activation(
+                look[:], e[g][:].indirect(p1[:]), ACT.Exp, bias=bias[:, g:g + 1], scale=temp_sb[:, g:g + 1])
+            return look
+
+        def join(g, look):
+            capped = ring([P, PICK], F32, "capped", 4)
+            nc.vector.scalar_tensor_tensor(
+                capped[:], look[:], gain_sb[:, g:g + 1], lim_sb[:, g, :], ALU.mult, ALU.min)
+            pair = held([P, PICK], F32, "pair%d" % g)
+            nc.vector.tensor_tensor(pair[:], e[g][:].indirect(p2[:]), capped[:], ALU.mult)
+            nc.sync.dma_start(out[g * P:(g + 1) * P, :], pair[:])
+
+        residual(0, 0)
+        residual(0, 1)
+        tab2 = {}
+        quantise_w1(0, 0, round_w1(0, 0, nc.vector.tensor_copy, 1))
+        tab2[0] = placed([P, T3], U32, "tab2_0", 34)
+        load_words(tab2_words, 0, tab2[0])
+        quantise_w1(1, 0, round_w1(1, 0, nc.vector.tensor_copy, 1))
+        tab2[1] = placed([P, T3], U32, "tab2_1", 0)
+        load_words(tab2_words, 1, tab2[1])
+        features(0, 0)
+        late = [round_w1(0, 1, nc.scalar.copy, 4)]
+        lim_sb = placed([P, 4, PICK], F32, "lim_sb", 8)
+        nc.sync.dma_start(lim_sb[:], lim.rearrange("(g p) n -> p g n", p=P))
+        late.append(round_w1(1, 1, nc.scalar.copy, 4))
+        features(0, 1)
+        for a in range(2):
+            quantise_w1(a, 1, late[a])
+        residual(1, 0)
+        residual(1, 1)
+        features(1, 0)
+        v2_sc = held([P, S2], U8, "v2_sc")
+        nc.vector.tensor_copy(v2_sc[:], tab2_sc[:].indirect(idx2[:]))
+        gather_drafts(0)
+        gather_drafts(1)
+        for g in range(4):
+            scores(g, 0)
+        features(1, 1)
+        looks = []
+        for g in range(4):
+            scores(g, 1)
+            looks.append(finish(g))
+        for g in range(4):
+            join(g, looks[g])

@@ -42,11 +42,13 @@ def tile_list_clause_draft_scores_kernel(
         def placed(shape, dtype, name, kib):
             return shared.tile(shape, dtype, name=name, align_bytes=64, offset=kib * 1024)
 
-        w4_raw = placed([P, 2 * 2 * H], U8, "w4_raw", 16)
+        w4_raw = placed([P, 2 * 2 * H], U8, "w4_raw", 38)
         nc.sync.dma_start(
             w4_raw[:].bitcast(I32).rearrange("p (a c) -> p a c", a=2),
             w4_words.bitcast(I32).rearrange("a p c -> p a c"),
         )
+        tab_sc = held([P, T], U8, "tab_sc")
+        nc.sync.dma_start(tab_sc[96:, :].bitcast(I32), tab_scales.rearrange("a q t -> (a q) t").bitcast(I32))
         idx = keep.tile([P, S // 16], U16, name="idx")
         nc.sync.dma_start(idx[:], offs)
         idx2 = keep.tile([P, S2 // 16], U16, name="idx2")
@@ -56,36 +58,31 @@ def tile_list_clause_draft_scores_kernel(
         p2 = keep.tile([P, PICK // 16], U16, name="p2")
         nc.sync.dma_start(p2[:], pos2)
 
-        temp_sb = held([P, 4], F32, "temp_sb")
-        gain_sb = held([P, 4], F32, "gain_sb")
-        with nc.allow_non_contiguous_dma(reason="one value a row"):
-            nc.sync.dma_start(temp_sb[:], temp.rearrange("(g p) -> p g", p=P))
-            nc.sync.dma_start(gain_sb[:], gain.rearrange("(g p) -> p g", p=P))
-
         def load_words(words, a, tile):
             nc.sync.dma_start(tile[:].bitcast(I32), words[a].rearrange("p t i -> p (t i)").bitcast(I32))
 
-        def load_w1(a, b, kib):
-            raw = placed([P, PACK, PASS], F32, "w1_raw%d%d" % (a, b), kib)
-            rows = w1[a * PASS:(a + 1) * PASS, b * PASS:(b + 1) * PASS]
-            nc.sync.dma_start(raw[:], rows.rearrange("(p j) c -> p j c", j=PACK))
-            return raw
+        def load_w1(a, b, places):
+            pieces = len(places)
+            width = PASS // pieces
+            tiles = []
+            for s in range(pieces):
+                raw = placed([P, PACK, width], F32, "w1_raw%d%d%d" % (a, b, s), places[s])
+                c0 = b * PASS + s * width
+                rows = w1[a * PASS:(a + 1) * PASS, c0:c0 + width]
+                nc.sync.dma_start(raw[:], rows.rearrange("(p j) c -> p j c", j=PACK))
+                tiles.append(raw)
+            return tiles
 
-        tab = {0: placed([P, T], U32, "tab0", 0)}
+        tab = {0: placed([P, T], U32, "tab0", 8)}
         load_words(tab_words, 0, tab[0])
 
-        tab_sc = placed([P, T], U8, "tab_sc", 40)
         w4_sc_raw = held([P, 2 * H], U8, "w4_sc_raw")
-        v_sc1 = held([P, S], U8, "v_sc1")
-        nc.gpsimd.memset(w4_sc_raw[64:, :].bitcast(I32), 0)
-        nc.vector.memset(tab_sc[:].bitcast(I32), 0)
-        nc.vector.memset(w4_sc_raw[:64, :].bitcast(I32), 0)
-        nc.vector.memset(v_sc1[:].bitcast(I32), 0)
+        v_sc = held([P, 2 * S], U8, "v_sc")
+        nc.vector.memset(tab_sc[:96, :].bitcast(I32), 0)
+        nc.vector.memset(w4_sc_raw[:].bitcast(I32), 0)
+        nc.vector.memset(v_sc[:].bitcast(I32), 0)
         for q in range(QUADS):
             nc.scalar.dma_start(
-                tab_sc[32 * q:32 * q + 8, :].bitcast(I32), tab_scales[:, 4 * q:4 * q + 4, :].bitcast(I32))
-        for q in range(QUADS):
-            (nc.scalar if q < 2 else nc.gpsimd).dma_start(
                 w4_sc_raw[32 * q:32 * q + 4, :].bitcast(I32).rearrange("p (a c) -> p a c", a=2),
                 w4_scales[:, 4 * q:4 * q + 4, :].bitcast(I32).rearrange("a q c -> q a c"))
 
@@ -93,40 +90,40 @@ def tile_list_clause_draft_scores_kernel(
         nc.vector.tensor_copy(
             w4[:].bitcast(U16).rearrange("p (g t m) -> p g t m", t=PACK, m=P),
             w4_raw[:].bitcast(U16).rearrange("p (g m t) -> p g t m", t=PACK, m=P))
-        tab[1] = placed([P, T], U32, "tab1", 16)
+        tab[1] = placed([P, T], U32, "tab1", 24)
         load_words(tab_words, 1, tab[1])
-        v_sc = held([P, S], U8, "v_sc")
-        nc.vector.tensor_copy(v_sc[:], tab_sc[:].indirect(idx[:]))
-        nc.scalar.dma_start(v_sc1[0:100, :].bitcast(I32), v_sc[4:104, :].bitcast(I32))
+        v_sc_rows = placed([P, S], U8, "v_sc_rows", 41)
+        nc.vector.tensor_copy(v_sc_rows[:], tab_sc[:].indirect(idx[:]))
+        for a in range(2):
+            for q in range(QUADS):
+                r0 = 96 + 16 * a + 4 * q
+                (nc.gpsimd if a == 1 and q >= 2 else nc.scalar).dma_start(
+                    v_sc[32 * q:32 * q + 4, a * S:(a + 1) * S].bitcast(I32), v_sc_rows[r0:r0 + 4, :].bitcast(I32))
+
         w4_sc = held([P, 2 * H], U8, "w4_sc")
         nc.vector.tensor_copy(
             w4_sc[:].rearrange("p (g t m) -> p g t m", t=PACK, m=P),
             w4_sc_raw[:].rearrange("p (g m t) -> p g t m", t=PACK, m=P))
-
-        v0 = placed([P, S], U32, "v0", 42)
+        v0 = held([P, S], U32, "v0")
         nc.vector.tensor_copy(v0[:], tab[0][:].indirect(idx[:]))
         v = {(0, u): v0[:, u * BANK:(u + 1) * BANK] for u in range(2)}
-        w1_raw = {(0, 0): load_w1(0, 0, 34), (1, 0): load_w1(1, 0, 0), (0, 1): load_w1(0, 1, 8)}
+        w1_raw = {(0, 0): load_w1(0, 0, (16,)), (1, 0): load_w1(1, 0, (8, 12))}
         for u in range(2):
             v1 = held([P, BANK], U32, "v1_%d" % u)
             nc.vector.tensor_copy(v1[:], tab[1][:].indirect(idx[:, 32 * u:32 * (u + 1)]))
             v[1, u] = v1[:]
-        w1_raw[1, 1] = load_w1(1, 1, 16)
-        tab2_sc = placed([P, T3], U8, "tab2_sc", 24)
-        nc.gpsimd.memset(tab2_sc[:].bitcast(I32), 0)
-        for q in range(QUADS):
-            nc.sync.dma_start(
-                tab2_sc[32 * q:32 * q + 8, :].bitcast(I32), tab2_scales[:, 4 * q:4 * q + 4, :].bitcast(I32))
 
         w1_q, w1_sc = {}, {}
 
         def round_w1(a, b, engine_copy, pieces):
-            wb = ring([P, PACK * PASS], BF16, "w1_bf", 4)
-            dst = wb[:].rearrange("p (t m j) -> p m j t", t=PACK, j=PACK)
-            src = w1_raw[a, b][:].rearrange("p j (m t) -> p m j t", t=PACK)
+            wb = placed([P, PACK * PASS], BF16, "w1_bf%d%d" % (a, b), (24 + 4 * a) if b == 0 else (40 + 4 * a))
+            dst = wb[:].rearrange("p (t m j) -> p m t j", t=PACK, j=PACK)
             step = P // pieces
+            per_tile = pieces // len(w1_raw[a, b])
             for s in range(pieces):
-                engine_copy(dst[:, s * step:(s + 1) * step], src[:, s * step:(s + 1) * step])
+                src = w1_raw[a, b][s // per_tile][:].rearrange("p j (m t) -> p m t j", t=PACK)
+                m0 = (s % per_tile) * step
+                engine_copy(dst[:, s * step:(s + 1) * step], src[:, m0:m0 + step])
             return wb
 
         def quantise_w1(a, b, wb):
@@ -135,7 +132,7 @@ def tile_list_clause_draft_scores_kernel(
             nc.vector.quantize_mx(w1_q[a, b][:].bitcast(FP8X4), w1_sc[a, b][:], wb[:])
 
         res = {}
-        ROUNDED = ((0, 1), (1, 0), (1, 1))
+        ROUNDED = ((1, 0), (1, 1))
 
         def packed_bank(b, u, s, weight):
             bank = psum.tile([P, PACK, P], F32, name="packed_bank", tag="bank", bufs=8)
@@ -151,12 +148,11 @@ def tile_list_clause_draft_scores_kernel(
 
         def w1_operands(a, b, t, j0):
             return (w1_q[a, b][:, t * P:(t + 1) * P].bitcast(FP8X4), w1_sc[a, b][:, t * P:(t + 1) * P],
-                    v_sc[4 * a:, j0:j0 + P])
+                    v_sc[:, a * S + j0:a * S + j0 + P])
 
         def w4_operands(a, b, t, j0, width=P):
             c0 = ((2 * a + b) * PACK + t) * P
-            plane = v_sc if a == 0 else v_sc1
-            return w4[:, 2 * c0:2 * (c0 + P)].bitcast(FP4X4), w4_sc[:, c0:c0 + P], plane[:, j0:j0 + width]
+            return w4[:, 2 * c0:2 * (c0 + P)].bitcast(FP4X4), w4_sc[:, c0:c0 + P], v_sc[:, a * S + j0:a * S + j0 + width]
 
         def rounded(b, u, weight, name):
             tile = ring([P, PACK * BANK], BF16, name, 3)
@@ -171,7 +167,7 @@ def tile_list_clause_draft_scores_kernel(
             if (b, u) in ROUNDED:
                 res[b, u] = rounded(b, u, w4_operands, "res_bf")
                 return
-            res[b, u] = held([P, PACK, BANK], F32, "res%d%d" % (b, u))
+            res[b, u] = placed([P, PACK, BANK], F32, "res%d%d" % (b, u), 48 + 8 * u)
             for t in range(PACK):
                 bank = psum.tile([P, BANK], F32, name="res_bank", tag="bank", bufs=8)
                 for a in range(2):
@@ -194,9 +190,9 @@ def tile_list_clause_draft_scores_kernel(
                 for s in range(BANK // P):
                     bank = packed_bank(b, u, s, w1_operands)
                     nc.vector.tensor_tensor(
-                        hb[:, s * BANK:(s + 1) * BANK].rearrange("p (c i t) -> p c t i", i=4, t=PACK),
-                        bank[:].rearrange("p t (c i) -> p c t i", i=4),
-                        res[b, u][:, :, s * P:(s + 1) * P].rearrange("p t (c i) -> p c t i", i=4),
+                        hb[:, s * BANK:(s + 1) * BANK].rearrange("p (c i t) -> p c t i", i=2, t=PACK),
+                        bank[:].rearrange("p t (c i) -> p c t i", i=2),
+                        res[b, u][:, :, s * P:(s + 1) * P].rearrange("p t (c i) -> p c t i", i=2),
                         ALU.max)
             h_q[b, u] = held([P, BANK], U32, "h_q%d%d" % (b, u))
             h_sc[b, u] = held([P, BANK], U8, "h_sc%d%d" % (b, u))
@@ -244,19 +240,30 @@ def tile_list_clause_draft_scores_kernel(
         residual(0, 1)
         tab2 = {}
         quantise_w1(0, 0, round_w1(0, 0, nc.vector.tensor_copy, 1))
-        tab2[0] = placed([P, T3], U32, "tab2_0", 34)
-        load_words(tab2_words, 0, tab2[0])
-        quantise_w1(1, 0, round_w1(1, 0, nc.vector.tensor_copy, 1))
-        tab2[1] = placed([P, T3], U32, "tab2_1", 0)
-        load_words(tab2_words, 1, tab2[1])
+        w1_raw[0, 1] = load_w1(0, 1, (16,))
+        quantise_w1(1, 0, round_w1(1, 0, nc.vector.tensor_copy, 2))
+        w1_raw[1, 1] = load_w1(1, 1, (4,))
+        tab2_sc = placed([P, T3], U8, "tab2_sc", 28)
+        nc.gpsimd.memset(tab2_sc[:].bitcast(I32), 0)
+        for q in range(QUADS):
+            nc.sync.dma_start(
+                tab2_sc[32 * q:32 * q + 8, :].bitcast(I32), tab2_scales[:, 4 * q:4 * q + 4, :].bitcast(I32))
         features(0, 0)
-        late = [round_w1(0, 1, nc.scalar.copy, 4)]
-        lim_sb = placed([P, 4, PICK], F32, "lim_sb", 8)
+        tab2[0] = placed([P, T3], U32, "tab2_0", 48)
+        load_words(tab2_words, 0, tab2[0])
+        late = [round_w1(a, 1, nc.scalar.copy, 4) for a in range(2)]
+        lim_sb = placed([P, 4, PICK], F32, "lim_sb", 4)
         nc.sync.dma_start(lim_sb[:], lim.rearrange("(g p) n -> p g n", p=P))
-        late.append(round_w1(1, 1, nc.scalar.copy, 4))
         features(0, 1)
+        tab2[1] = placed([P, T3], U32, "tab2_1", 56)
+        load_words(tab2_words, 1, tab2[1])
         for a in range(2):
             quantise_w1(a, 1, late[a])
+        temp_sb = placed([P, 4], F32, "temp_sb", 40)
+        gain_sb = placed([P, 4], F32, "gain_sb", 41)
+        with nc.allow_non_contiguous_dma(reason="one value a row"):
+            nc.sync.dma_start(temp_sb[:], temp.rearrange("(g p) -> p g", p=P))
+            nc.sync.dma_start(gain_sb[:], gain.rearrange("(g p) -> p g", p=P))
         residual(1, 0)
         residual(1, 1)
         features(1, 0)

@@ -42,7 +42,7 @@ def tile_list_clause_draft_scores_kernel(
         def placed(shape, dtype, name, kib):
             return shared.tile(shape, dtype, name=name, align_bytes=64, offset=kib * 1024)
 
-        w4_raw = placed([P, 2 * 2 * H], U8, "w4_raw", 38)
+        w4_raw = placed([P, 2 * 2 * H], U8, "w4_raw", 40)
         nc.sync.dma_start(
             w4_raw[:].bitcast(I32).rearrange("p (a c) -> p a c", a=2),
             w4_words.bitcast(I32).rearrange("a p c -> p a c"),
@@ -76,11 +76,12 @@ def tile_list_clause_draft_scores_kernel(
         tab = {0: placed([P, T], U32, "tab0", 8)}
         load_words(tab_words, 0, tab[0])
 
-        w4_sc_raw = held([P, 2 * H], U8, "w4_sc_raw")
-        v_sc = held([P, 2 * S], U8, "v_sc")
+        w4_sc_raw = placed([P, 2 * H], U8, "w4_sc_raw", 70)
+        v_sc = [held([P, S], U8, "v_sc%d" % a) for a in range(2)]
         nc.vector.memset(tab_sc[:96, :].bitcast(I32), 0)
         nc.vector.memset(w4_sc_raw[:].bitcast(I32), 0)
-        nc.vector.memset(v_sc[:].bitcast(I32), 0)
+        for a in range(2):
+            nc.gpsimd.memset(v_sc[a][:].bitcast(I32), 0)
         for q in range(QUADS):
             nc.scalar.dma_start(
                 w4_sc_raw[32 * q:32 * q + 4, :].bitcast(I32).rearrange("p (a c) -> p a c", a=2),
@@ -90,33 +91,33 @@ def tile_list_clause_draft_scores_kernel(
         nc.vector.tensor_copy(
             w4[:].bitcast(U16).rearrange("p (g t m) -> p g t m", t=PACK, m=P),
             w4_raw[:].bitcast(U16).rearrange("p (g m t) -> p g t m", t=PACK, m=P))
-        tab[1] = placed([P, T], U32, "tab1", 24)
+        tab[1] = placed([P, T], U32, "tab1", 26)
         load_words(tab_words, 1, tab[1])
-        v_sc_rows = placed([P, S], U8, "v_sc_rows", 41)
+        v_sc_rows = placed([P, S], U8, "v_sc_rows", 43)
         nc.vector.tensor_copy(v_sc_rows[:], tab_sc[:].indirect(idx[:]))
         for a in range(2):
             for q in range(QUADS):
                 r0 = 96 + 16 * a + 4 * q
                 (nc.gpsimd if a == 1 and q >= 2 else nc.scalar).dma_start(
-                    v_sc[32 * q:32 * q + 4, a * S:(a + 1) * S].bitcast(I32), v_sc_rows[r0:r0 + 4, :].bitcast(I32))
+                    v_sc[a][32 * q:32 * q + 4, :].bitcast(I32), v_sc_rows[r0:r0 + 4, :].bitcast(I32))
 
-        w4_sc = held([P, 2 * H], U8, "w4_sc")
-        nc.vector.tensor_copy(
-            w4_sc[:].rearrange("p (g t m) -> p g t m", t=PACK, m=P),
-            w4_sc_raw[:].rearrange("p (g m t) -> p g t m", t=PACK, m=P))
         v0 = held([P, S], U32, "v0")
         nc.vector.tensor_copy(v0[:], tab[0][:].indirect(idx[:]))
         v = {(0, u): v0[:, u * BANK:(u + 1) * BANK] for u in range(2)}
-        w1_raw = {(0, 0): load_w1(0, 0, (16,)), (1, 0): load_w1(1, 0, (8, 12))}
+        w1_raw = {(0, 0): load_w1(0, 0, (18,)), (1, 0): load_w1(1, 0, (10, 14))}
+        w4_sc = placed([P, 2 * H], U8, "w4_sc", 8)
+        nc.vector.tensor_copy(
+            w4_sc[:].rearrange("p (g t m) -> p g t m", t=PACK, m=P),
+            w4_sc_raw[:].rearrange("p (g m t) -> p g t m", t=PACK, m=P))
         for u in range(2):
-            v1 = held([P, BANK], U32, "v1_%d" % u)
+            v1 = placed([P, BANK], U32, "v1_%d" % u, 71 - 2 * u)
             nc.vector.tensor_copy(v1[:], tab[1][:].indirect(idx[:, 32 * u:32 * (u + 1)]))
             v[1, u] = v1[:]
 
         w1_q, w1_sc = {}, {}
 
         def round_w1(a, b, engine_copy, pieces):
-            wb = placed([P, PACK * PASS], BF16, "w1_bf%d%d" % (a, b), (24 + 4 * a) if b == 0 else (40 + 4 * a))
+            wb = placed([P, PACK * PASS], BF16, "w1_bf%d%d" % (a, b), (26 + 6 * a) if b == 0 else (44 + 20 * a))
             dst = wb[:].rearrange("p (t m j) -> p m t j", t=PACK, j=PACK)
             step = P // pieces
             per_tile = pieces // len(w1_raw[a, b])
@@ -134,8 +135,8 @@ def tile_list_clause_draft_scores_kernel(
         res = {}
         ROUNDED = ((1, 0), (1, 1))
 
-        def packed_bank(b, u, s, weight):
-            bank = psum.tile([P, PACK, P], F32, name="packed_bank", tag="bank", bufs=8)
+        def packed_bank(b, u, s, weight, tag):
+            bank = psum.tile([P, PACK, P], F32, name="packed_bank", tag=tag, bufs=4)
             j0 = u * BANK + s * P
             for a in range(2):
                 for t in range(PACK):
@@ -148,16 +149,16 @@ def tile_list_clause_draft_scores_kernel(
 
         def w1_operands(a, b, t, j0):
             return (w1_q[a, b][:, t * P:(t + 1) * P].bitcast(FP8X4), w1_sc[a, b][:, t * P:(t + 1) * P],
-                    v_sc[:, a * S + j0:a * S + j0 + P])
+                    v_sc[a][:, j0:j0 + P])
 
         def w4_operands(a, b, t, j0, width=P):
             c0 = ((2 * a + b) * PACK + t) * P
-            return w4[:, 2 * c0:2 * (c0 + P)].bitcast(FP4X4), w4_sc[:, c0:c0 + P], v_sc[:, a * S + j0:a * S + j0 + width]
+            return w4[:, 2 * c0:2 * (c0 + P)].bitcast(FP4X4), w4_sc[:, c0:c0 + P], v_sc[a][:, j0:j0 + width]
 
         def rounded(b, u, weight, name):
             tile = ring([P, PACK * BANK], BF16, name, 3)
             for s in range(BANK // P):
-                bank = packed_bank(b, u, s, weight)
+                bank = packed_bank(b, u, s, weight, name + "_bank")
                 nc.scalar.copy(
                     tile[:, s * BANK:(s + 1) * BANK].rearrange("p (j t) -> p j t", t=PACK),
                     bank[:].rearrange("p t j -> p j t"))
@@ -169,7 +170,7 @@ def tile_list_clause_draft_scores_kernel(
                 return
             res[b, u] = placed([P, PACK, BANK], F32, "res%d%d" % (b, u), 48 + 8 * u)
             for t in range(PACK):
-                bank = psum.tile([P, BANK], F32, name="res_bank", tag="bank", bufs=8)
+                bank = psum.tile([P, BANK], F32, name="res_bank", tag="res_bf_bank", bufs=4)
                 for a in range(2):
                     lhsT, lhsT_scale, rhs_scale = w4_operands(a, b, t, u * BANK, BANK)
                     nc.tensor.matmul_mx(
@@ -188,7 +189,7 @@ def tile_list_clause_draft_scores_kernel(
                     nc.vector.tensor_tensor(hb[:, cols], f[:, cols], res[b, u][:, cols], ALU.max)
             else:
                 for s in range(BANK // P):
-                    bank = packed_bank(b, u, s, w1_operands)
+                    bank = packed_bank(b, u, s, w1_operands, "f_bf_bank")
                     nc.vector.tensor_tensor(
                         hb[:, s * BANK:(s + 1) * BANK].rearrange("p (c i t) -> p c t i", i=2, t=PACK),
                         bank[:].rearrange("p t (c i) -> p c t i", i=2),
@@ -209,7 +210,7 @@ def tile_list_clause_draft_scores_kernel(
         bias = held([P, 4], F32, "bias")
 
         def scores(g, u):
-            bank = psum.tile([P, BANK], F32, name="e_bank", tag="bank", bufs=8)
+            bank = psum.tile([P, BANK], F32, name="e_bank", tag="res_bf_bank", bufs=4)
             for b in range(2):
                 nc.tensor.matmul_mx(
                     bank[:], lhsT=v2[b][:, g * P:(g + 1) * P].bitcast(FP8X4),
@@ -240,37 +241,36 @@ def tile_list_clause_draft_scores_kernel(
         residual(0, 1)
         tab2 = {}
         quantise_w1(0, 0, round_w1(0, 0, nc.vector.tensor_copy, 1))
-        w1_raw[0, 1] = load_w1(0, 1, (16,))
+        w1_raw[0, 1] = load_w1(0, 1, (18,))
         quantise_w1(1, 0, round_w1(1, 0, nc.vector.tensor_copy, 2))
-        w1_raw[1, 1] = load_w1(1, 1, (4,))
-        tab2_sc = placed([P, T3], U8, "tab2_sc", 28)
+        w1_raw[1, 1] = load_w1(1, 1, (10,))
+        for a in range(2):
+            tab2[a] = placed([P, T3], U32, "tab2_%d" % a, 26 + 8 * a)
+            load_words(tab2_words, a, tab2[a])
+        features(0, 0)
+        tab2_sc = placed([P, T3], U8, "tab2_sc", 48)
         nc.gpsimd.memset(tab2_sc[:].bitcast(I32), 0)
         for q in range(QUADS):
             nc.sync.dma_start(
                 tab2_sc[32 * q:32 * q + 8, :].bitcast(I32), tab2_scales[:, 4 * q:4 * q + 4, :].bitcast(I32))
-        features(0, 0)
-        tab2[0] = placed([P, T3], U32, "tab2_0", 48)
-        load_words(tab2_words, 0, tab2[0])
         late = [round_w1(a, 1, nc.scalar.copy, 4) for a in range(2)]
-        lim_sb = placed([P, 4, PICK], F32, "lim_sb", 4)
+        lim_sb = placed([P, 4, PICK], F32, "lim_sb", 10)
         nc.sync.dma_start(lim_sb[:], lim.rearrange("(g p) n -> p g n", p=P))
         features(0, 1)
-        tab2[1] = placed([P, T3], U32, "tab2_1", 56)
-        load_words(tab2_words, 1, tab2[1])
         for a in range(2):
             quantise_w1(a, 1, late[a])
-        temp_sb = placed([P, 4], F32, "temp_sb", 40)
-        gain_sb = placed([P, 4], F32, "gain_sb", 41)
+        temp_sb = placed([P, 4], F32, "temp_sb", 44)
+        gain_sb = placed([P, 4], F32, "gain_sb", 45)
         with nc.allow_non_contiguous_dma(reason="one value a row"):
             nc.sync.dma_start(temp_sb[:], temp.rearrange("(g p) -> p g", p=P))
             nc.sync.dma_start(gain_sb[:], gain.rearrange("(g p) -> p g", p=P))
         residual(1, 0)
         residual(1, 1)
         features(1, 0)
-        v2_sc = held([P, S2], U8, "v2_sc")
-        nc.vector.tensor_copy(v2_sc[:], tab2_sc[:].indirect(idx2[:]))
         gather_drafts(0)
         gather_drafts(1)
+        v2_sc = held([P, S2], U8, "v2_sc")
+        nc.vector.tensor_copy(v2_sc[:], tab2_sc[:].indirect(idx2[:]))
         for g in range(4):
             scores(g, 0)
         features(1, 1)

@@ -42,15 +42,15 @@ def tile_list_clause_draft_scores_kernel(
         def placed(shape, dtype, name, kib):
             return shared.tile(shape, dtype, name=name, align_bytes=64, offset=kib * 1024)
 
-        w4_raw = placed([P, 2 * 2 * H], U8, "w4_raw", 40)
+        tab_sc = placed([P, T], U8, "tab_sc", 40)
+        nc.sync.dma_start(tab_sc[96:, :].bitcast(I32), tab_scales.rearrange("a q t -> (a q) t").bitcast(I32))
+        idx = keep.tile([P, S // 16], U16, name="idx")
+        nc.sync.dma_start(idx[:], offs)
+        w4_raw = held([P, 2 * 2 * H], U8, "w4_raw")
         nc.sync.dma_start(
             w4_raw[:].bitcast(I32).rearrange("p (a c) -> p a c", a=2),
             w4_words.bitcast(I32).rearrange("a p c -> p a c"),
         )
-        tab_sc = held([P, T], U8, "tab_sc")
-        nc.sync.dma_start(tab_sc[96:, :].bitcast(I32), tab_scales.rearrange("a q t -> (a q) t").bitcast(I32))
-        idx = keep.tile([P, S // 16], U16, name="idx")
-        nc.sync.dma_start(idx[:], offs)
         idx2 = keep.tile([P, S2 // 16], U16, name="idx2")
         nc.sync.dma_start(idx2[:], offs2)
         p1 = keep.tile([P, PICK // 16], U16, name="p1")
@@ -83,24 +83,24 @@ def tile_list_clause_draft_scores_kernel(
         for a in range(2):
             nc.gpsimd.memset(v_sc[a][:].bitcast(I32), 0)
         for q in range(QUADS):
-            nc.scalar.dma_start(
+            nc.sync.dma_start(
                 w4_sc_raw[32 * q:32 * q + 4, :].bitcast(I32).rearrange("p (a c) -> p a c", a=2),
                 w4_scales[:, 4 * q:4 * q + 4, :].bitcast(I32).rearrange("a q c -> q a c"))
 
-        w4 = held([P, 2 * 2 * H], U8, "w4")
-        nc.vector.tensor_copy(
-            w4[:].bitcast(U16).rearrange("p (g t m) -> p g t m", t=PACK, m=P),
-            w4_raw[:].bitcast(U16).rearrange("p (g m t) -> p g t m", t=PACK, m=P))
+        v_sc_rows = held([P, S], U8, "v_sc_rows")
+        nc.vector.tensor_copy(v_sc_rows[:], tab_sc[:].indirect(idx[:]))
         tab[1] = placed([P, T], U32, "tab1", 26)
         load_words(tab_words, 1, tab[1])
-        v_sc_rows = placed([P, S], U8, "v_sc_rows", 43)
-        nc.vector.tensor_copy(v_sc_rows[:], tab_sc[:].indirect(idx[:]))
         for a in range(2):
             for q in range(QUADS):
                 r0 = 96 + 16 * a + 4 * q
-                (nc.gpsimd if a == 1 and q >= 2 else nc.scalar).dma_start(
+                (nc.gpsimd if a == 1 and q >= 2 else nc.sync).dma_start(
                     v_sc[a][32 * q:32 * q + 4, :].bitcast(I32), v_sc_rows[r0:r0 + 4, :].bitcast(I32))
 
+        w4 = placed([P, 2 * 2 * H], U8, "w4", 42)
+        nc.vector.tensor_copy(
+            w4[:].bitcast(U16).rearrange("p (g t m) -> p g t m", t=PACK, m=P),
+            w4_raw[:].bitcast(U16).rearrange("p (g m t) -> p g t m", t=PACK, m=P))
         v0 = held([P, S], U32, "v0")
         nc.vector.tensor_copy(v0[:], tab[0][:].indirect(idx[:]))
         v = {(0, u): v0[:, u * BANK:(u + 1) * BANK] for u in range(2)}
@@ -117,7 +117,7 @@ def tile_list_clause_draft_scores_kernel(
         w1_q, w1_sc = {}, {}
 
         def round_w1(a, b, engine_copy, pieces):
-            wb = placed([P, PACK * PASS], BF16, "w1_bf%d%d" % (a, b), (26 + 6 * a) if b == 0 else (44 + 20 * a))
+            wb = placed([P, PACK * PASS], BF16, "w1_bf%d%d" % (a, b), (26 + 6 * a) if b == 0 else (74 - 10 * a))
             dst = wb[:].rearrange("p (t m j) -> p m t j", t=PACK, j=PACK)
             step = P // pieces
             per_tile = pieces // len(w1_raw[a, b])
@@ -259,8 +259,8 @@ def tile_list_clause_draft_scores_kernel(
         features(0, 1)
         for a in range(2):
             quantise_w1(a, 1, late[a])
-        temp_sb = placed([P, 4], F32, "temp_sb", 44)
-        gain_sb = placed([P, 4], F32, "gain_sb", 45)
+        temp_sb = placed([P, 4], F32, "temp_sb", 74)
+        gain_sb = placed([P, 4], F32, "gain_sb", 75)
         with nc.allow_non_contiguous_dma(reason="one value a row"):
             nc.sync.dma_start(temp_sb[:], temp.rearrange("(g p) -> p g", p=P))
             nc.sync.dma_start(gain_sb[:], gain.rearrange("(g p) -> p g", p=P))

from contextlib import ExitStack

import concourse.mybir as mybir

K, T, S, H, T3, S2, PICK = 1024, 4096, 1024, 1024, 2048, 512, 512
FLOPS = 2 * 2 * K * H * S + 2 * H * S2 * S

F32 = mybir.dt.float32
BF16 = mybir.dt.bfloat16
I32 = mybir.dt.int32
U32 = mybir.dt.uint32
U16 = mybir.dt.uint16
U8 = mybir.dt.uint8
FP8X4 = mybir.dt.float8_e4m3fn_x4
FP4X4 = mybir.dt.float4_e2m1fn_x4
ALU = mybir.AluOpType
ACT = mybir.ActivationFunctionType

P = 128
PACK = 4
PASS = P * PACK
BANK = 512
QUADS = 4


def tile_list_clause_draft_scores_kernel(
    tc, tab_words, tab_scales, offs, tab2_words, tab2_scales, offs2, pos1, pos2,
    w1, w4_words, w4_scales, temp, gain, lim, out,
):
    nc = tc.nc
    with ExitStack() as ctx:
        keep = ctx.enter_context(tc.tile_pool(name="keep", bufs=1))
        shared = ctx.enter_context(tc.tile_pool(name="shared", bufs=1))
        psum = ctx.enter_context(tc.psum_pool(name="psum", bufs=1))

        def held(shape, dtype, name):
            return keep.tile(shape, dtype, name=name, align_bytes=64)

        def ring(shape, dtype, name, bufs):
            return keep.tile(shape, dtype, name=name, tag=name, bufs=bufs, align_bytes=64)

        def placed(shape, dtype, name, kib):
            return shared.tile(shape, dtype, name=name, align_bytes=64, offset=kib * 1024)

        tab_sc = placed([P, T], U8, "tab_sc", 40)
        nc.sync.dma_start(tab_sc[96:, :].bitcast(I32), tab_scales.rearrange("a q t -> (a q) t").bitcast(I32))
        idx = keep.tile([P, S // 16], U16, name="idx")
        nc.sync.dma_start(idx[:], offs)
        w4_raw = held([P, 2 * 2 * H], U8, "w4_raw")
        nc.sync.dma_start(
            w4_raw[:].bitcast(I32).rearrange("p (a c) -> p a c", a=2),
            w4_words.bitcast(I32).rearrange("a p c -> p a c"),
        )
        idx2 = keep.tile([P, S2 // 16], U16, name="idx2")
        nc.sync.dma_start(idx2[:], offs2)
        p1 = keep.tile([P, PICK // 16], U16, name="p1")
        nc.sync.dma_start(p1[:], pos1)
        p2 = keep.tile([P, PICK // 16], U16, name="p2")
        nc.sync.dma_start(p2[:], pos2)

        def load_words(words, a, tile):
            nc.sync.dma_start(tile[:].bitcast(I32), words[a].rearrange("p t i -> p (t i)").bitcast(I32))

        def load_w1(a, b, places):
            pieces = len(places)
            width = PASS // pieces
            tiles = []
            for s in range(pieces):
                raw = placed([P, PACK, width], F32, "w1_raw%d%d%d" % (a, b, s), places[s])
                c0 = b * PASS + s * width
                rows = w1[a * PASS:(a + 1) * PASS, c0:c0 + width]
                nc.sync.dma_start(raw[:], rows.rearrange("(p j) c -> p j c", j=PACK))
                tiles.append(raw)
            return tiles

        tab = {0: placed([P, T], U32, "tab0", 8)}
        load_words(tab_words, 0, tab[0])

        w4_sc_raw = placed([P, 2 * H], U8, "w4_sc_raw", 70)
        v_sc = [held([P, S], U8, "v_sc%d" % a) for a in range(2)]
        nc.vector.memset(tab_sc[:96, :].bitcast(I32), 0)
        nc.vector.memset(w4_sc_raw[:].bitcast(I32), 0)
        for a in range(2):
            nc.gpsimd.memset(v_sc[a][:].bitcast(I32), 0)
        for q in range(QUADS):
            nc.sync.dma_start(
                w4_sc_raw[32 * q:32 * q + 4, :].bitcast(I32).rearrange("p (a c) -> p a c", a=2),
                w4_scales[:, 4 * q:4 * q + 4, :].bitcast(I32).rearrange("a q c -> q a c"))

        v_sc_rows = held([P, S], U8, "v_sc_rows")
        nc.vector.tensor_copy(v_sc_rows[:], tab_sc[:].indirect(idx[:]))
        tab[1] = placed([P, T], U32, "tab1", 26)
        load_words(tab_words, 1, tab[1])
        for a in range(2):
            for q in range(QUADS):
                r0 = 96 + 16 * a + 4 * q
                (nc.gpsimd if a == 1 and q >= 2 else nc.sync).dma_start(
                    v_sc[a][32 * q:32 * q + 4, :].bitcast(I32), v_sc_rows[r0:r0 + 4, :].bitcast(I32))

        w4 = placed([P, 2 * 2 * H], U8, "w4", 42)
        nc.vector.tensor_copy(
            w4[:].bitcast(U16).rearrange("p (g t m) -> p g t m", t=PACK, m=P),
            w4_raw[:].bitcast(U16).rearrange("p (g m t) -> p g t m", t=PACK, m=P))
        v0 = held([P, S], U32, "v0")
        nc.vector.tensor_copy(v0[:], tab[0][:].indirect(idx[:]))
        v = {(0, u): v0[:, u * BANK:(u + 1) * BANK] for u in range(2)}
        w1_raw = {(0, 0): load_w1(0, 0, (18,)), (1, 0): load_w1(1, 0, (10, 14))}
        w4_sc = placed([P, 2 * H], U8, "w4_sc", 8)
        nc.vector.tensor_copy(
            w4_sc[:].rearrange("p (g t m) -> p g t m", t=PACK, m=P),
            w4_sc_raw[:].rearrange("p (g m t) -> p g t m", t=PACK, m=P))
        for u in range(2):
            v1 = placed([P, BANK], U32, "v1_%d" % u, 71 - 2 * u)
            nc.vector.tensor_copy(v1[:], tab[1][:].indirect(idx[:, 32 * u:32 * (u + 1)]))
            v[1, u] = v1[:]

        w1_q, w1_sc = {}, {}

        def round_w1(a, b, engine_copy, pieces):
            wb = placed([P, PACK * PASS], BF16, "w1_bf%d%d" % (a, b), (26 + 6 * a) if b == 0 else (74 - 10 * a))
            dst = wb[:].rearrange("p (t m j) -> p m t j", t=PACK, j=PACK)
            step = P // pieces
            per_tile = pieces // len(w1_raw[a, b])
            for s in range(pieces):
                src = w1_raw[a, b][s // per_tile][:].rearrange("p j (m t) -> p m t j", t=PACK)
                m0 = (s % per_tile) * step
                engine_copy(dst[:, s * step:(s + 1) * step], src[:, m0:m0 + step])
            return wb

        def quantise_w1(a, b, wb):
            w1_q[a, b] = held([P, PASS], U32, "w1_q%d%d" % (a, b))
            w1_sc[a, b] = held([P, PASS], U8, "w1_sc%d%d" % (a, b))
            nc.vector.quantize_mx(w1_q[a, b][:].bitcast(FP8X4), w1_sc[a, b][:], wb[:])

        res = {}
        ROUNDED = ((1, 0), (1, 1))

        def packed_bank(b, u, s, weight, tag):
            bank = psum.tile([P, PACK, P], F32, name="packed_bank", tag=tag, bufs=4)
            j0 = u * BANK + s * P
            for a in range(2):
                for t in range(PACK):
                    lhsT, lhsT_scale, rhs_scale = weight(a, b, t, j0)
                    nc.tensor.matmul_mx(
                        bank[:, t, :], lhsT=lhsT, lhsT_scale=lhsT_scale,
                        rhs=v[a, u][:, s * P:(s + 1) * P].bitcast(FP8X4), rhs_scale=rhs_scale,
                        start=(a == 0 and t == 0), stop=(a == 1 and t == PACK - 1))
            return bank

        def w1_operands(a, b, t, j0):
            return (w1_q[a, b][:, t * P:(t + 1) * P].bitcast(FP8X4), w1_sc[a, b][:, t * P:(t + 1) * P],
                    v_sc[a][:, j0:j0 + P])

        def w4_operands(a, b, t, j0, width=P):
            c0 = ((2 * a + b) * PACK + t) * P
            return w4[:, 2 * c0:2 * (c0 + P)].bitcast(FP4X4), w4_sc[:, c0:c0 + P], v_sc[a][:, j0:j0 + width]

        def rounded(b, u, weight, name):
            tile = ring([P, PACK * BANK], BF16, name, 3)
            for s in range(BANK // P):
                bank = packed_bank(b, u, s, weight, name + "_bank")
                nc.scalar.copy(
                    tile[:, s * BANK:(s + 1) * BANK].rearrange("p (j t) -> p j t", t=PACK),
                    bank[:].rearrange("p t j -> p j t"))
            return tile

        def residual(b, u):
            if (b, u) in ROUNDED:
                res[b, u] = rounded(b, u, w4_operands, "res_bf")
                return
            res[b, u] = placed([P, PACK, BANK], F32, "res%d%d" % (b, u), 48 + 8 * u)
            for t in range(PACK):
                bank = psum.tile([P, BANK], F32, name="res_bank", tag="res_bf_bank", bufs=4)
                for a in range(2):
                    lhsT, lhsT_scale, rhs_scale = w4_operands(a, b, t, u * BANK, BANK)
                    nc.tensor.matmul_mx(
                        bank[:], lhsT=lhsT, lhsT_scale=lhsT_scale,
                        rhs=v[a, u].bitcast(FP8X4), rhs_scale=rhs_scale, start=(a == 0), stop=(a == 1))
                nc.scalar.copy(res[b, u][:, t, :], bank[:])

        h_q, h_sc = {}, {}

        def features(b, u):
            hb = ring([P, PACK * BANK], BF16, "h_bf", 3)
            if (b, u) in ROUNDED:
                f = rounded(b, u, w1_operands, "f_bf")
                for s in range(2):
                    cols = slice(s * 2 * BANK, (s + 1) * 2 * BANK)
                    nc.vector.tensor_tensor(hb[:, cols], f[:, cols], res[b, u][:, cols], ALU.max)
            else:
                for s in range(BANK // P):
                    bank = packed_bank(b, u, s, w1_operands, "f_bf_bank")
                    nc.vector.tensor_tensor(
                        hb[:, s * BANK:(s + 1) * BANK].rearrange("p (c i t) -> p c t i", i=2, t=PACK),
                        bank[:].rearrange("p t (c i) -> p c t i", i=2),
                        res[b, u][:, :, s * P:(s + 1) * P].rearrange("p t (c i) -> p c t i", i=2),
                        ALU.max)
            h_q[b, u] = held([P, BANK], U32, "h_q%d%d" % (b, u))
            h_sc[b, u] = held([P, BANK], U8, "h_sc%d%d" % (b, u))
            nc.vector.quantize_mx(h_q[b, u][:].bitcast(FP8X4), h_sc[b, u][:], hb[:])

        v2 = {}

        def gather_drafts(b):
            v2[b] = held([P, S2], U32, "v2_%d" % b)
            nc.vector.tensor_copy(v2[b][:], tab2[b][:].indirect(idx2[:]))

        e = [held([P, S], F32, "e%d" % g) for g in range(4)]
        top = [held([P, 4], F32, "top%d" % u) for u in range(2)]
        bias = held([P, 4], F32, "bias")

        def scores(g, u):
            bank = psum.tile([P, BANK], F32, name="e_bank", tag="res_bf_bank", bufs=4)
            for b in range(2):
                nc.tensor.matmul_mx(
                    bank[:], lhsT=v2[b][:, g * P:(g + 1) * P].bitcast(FP8X4),
                    lhsT_scale=v2_sc[4 * b:, g * P:(g + 1) * P],
                    rhs=h_q[b, u][:].bitcast(FP8X4), rhs_scale=h_sc[b, u][:],
                    start=(b == 0), stop=(b == 1))
            nc.vector.tensor_scalar(
                e[g][:, u * BANK:(u + 1) * BANK], bank[:], 1.0, top[0][:, g:g + 1] if u == 1 else None,
                ALU.mult, ALU.max, accum_out=top[u][:, g:g + 1])

        def finish(g):
            nc.vector.tensor_scalar(
                bias[:, g:g + 1], top[1][:, g:g + 1], temp_sb[:, g:g + 1], -1.0, ALU.mult, ALU.mult)
            look = held([P, PICK], F32, "look%d" % g)
            nc.scalar.activation(
                look[:], e[g][:].indirect(p1[:]), ACT.Exp, bias=bias[:, g:g + 1], scale=temp_sb[:, g:g + 1])
            return look

        def join(g, look):
            capped = ring([P, PICK], F32, "capped", 4)
            nc.vector.scalar_tensor_tensor(
                capped[:], look[:], gain_sb[:, g:g + 1], lim_sb[:, g, :], ALU.mult, ALU.min)
            pair = held([P, PICK], F32, "pair%d" % g)
            nc.vector.tensor_tensor(pair[:], e[g][:].indirect(p2[:]), capped[:], ALU.mult)
            nc.sync.dma_start(out[g * P:(g + 1) * P, :], pair[:])

        residual(0, 0)
        residual(0, 1)
        tab2 = {}
        quantise_w1(0, 0, round_w1(0, 0, nc.vector.tensor_copy, 1))
        w1_raw[0, 1] = load_w1(0, 1, (18,))
        quantise_w1(1, 0, round_w1(1, 0, nc.vector.tensor_copy, 2))
        w1_raw[1, 1] = load_w1(1, 1, (10,))
        for a in range(2):
            tab2[a] = placed([P, T3], U32, "tab2_%d" % a, 26 + 8 * a)
            load_words(tab2_words, a, tab2[a])
        features(0, 0)
        tab2_sc = placed([P, T3], U8, "tab2_sc", 48)
        nc.gpsimd.memset(tab2_sc[:].bitcast(I32), 0)
        for q in range(QUADS):
            nc.sync.dma_start(
                tab2_sc[32 * q:32 * q + 8, :].bitcast(I32), tab2_scales[:, 4 * q:4 * q + 4, :].bitcast(I32))
        late = [round_w1(a, 1, nc.scalar.copy, 4) for a in range(2)]
        lim_sb = placed([P, 4, PICK], F32, "lim_sb", 10)
        nc.sync.dma_start(lim_sb[:], lim.rearrange("(g p) n -> p g n", p=P))
        features(0, 1)
        for a in range(2):
            quantise_w1(a, 1, late[a])
        temp_sb = placed([P, 4], F32, "temp_sb", 74)
        gain_sb = placed([P, 4], F32, "gain_sb", 75)
        with nc.allow_non_contiguous_dma(reason="one value a row"):
            nc.sync.dma_start(temp_sb[:], temp.rearrange("(g p) -> p g", p=P))
            nc.sync.dma_start(gain_sb[:], gain.rearrange("(g p) -> p g", p=P))
        residual(1, 0)
        residual(1, 1)
        features(1, 0)
        gather_drafts(0)
        gather_drafts(1)
        v2_sc = held([P, S2], U8, "v2_sc")
        nc.vector.tensor_copy(v2_sc[:], tab2_sc[:].indirect(idx2[:]))
        for g in range(4):
            scores(g, 0)
        features(1, 1)
        looks = []
        for g in range(4):
            scores(g, 1)
            looks.append(finish(g))
        for g in range(4):
            join(g, looks[g])
